import numpy as np, ml_dtypes
CORES = [2,42,66,74,82,90,114]
N = 7
import mx_ref
NC, WT = 128, 3
BF = ml_dtypes.bfloat16
def pk(c, s, i=0):
    return (np.ascontiguousarray(c[:, 512 * i:512 * i + 512]), mx_ref.live(s[:, 128 * i:128 * i + 128]))
def inputs(rng, e, E):
    def f(*shape):
        v = (rng.standard_normal(shape, dtype=np.float32) * np.exp2(rng.integers(-2, 3, shape[:-1] + (1,)))).astype(BF)
        return mx_ref.spread((v.astype(np.float32) * np.exp2(rng.integers(-E, E + 1, shape[:-2] + (1, 1))).astype(np.float32)).astype(BF), rng, e)
    def packed(k):
        c = np.zeros((N, 128, k * 512), np.uint8); s = np.zeros((N, 128, k * 128), np.uint8)
        for r in range(N):
            for i in range(k):
                a, b = mx_ref.quantize(f(128, 512)); c[r][:, 512 * i:512 * i + 512] = a; s[r][:, 128 * i:128 * i + 128] = mx_ref.plane(b, rng)
        return c, s
    d = {}
    d["wc"], d["ws"] = packed(WT)
    d["x"] = f(N, 128, 4 * NC)
    return d
def setup_inputs(rng):
    return inputs(rng, 0, 0)
def setup_inputs_blocks(rng):
    return inputs(rng, 4, 0)
def setup_inputs_wide(rng):
    return inputs(rng, 0, 8)
def reference(wc, ws, x):
    y = np.zeros((N, 128, N * WT * NC), np.float32)
    for r in range(N):
        X = mx_ref.quantize(x[r])
        for b in range(N * WT):
            y[r][:, NC * b:NC * b + NC] = mx_ref.matmul(pk(wc[b // WT], ws[b // WT], b % WT), X)
    return {"y": y}

@@ -1,0 +1,147 @@
+from concourse.bass import DstId, RemoteDMATransfer
+from concourse.mybir import dt
+
+N = 7
+WT = 3
+NC = 128
+HW = WT * NC // 2
+BANKS = 8
+SLOTS = 2
+
+SCRATCH = {
+    "xb": ("sbuf", [128, 4 * NC], "bfloat16"),
+    "xq": ("sbuf", [128, NC], "float8_e4m3fn_x4"),
+    "xs": ("sbuf", [128, NC], "uint8"),
+    "wq": ("sbuf", [128, WT * NC], "float8_e4m3fn_x4"),
+    "wp": ("sbuf", [128, WT * NC], "uint8"),
+    "st": ("sbuf", [128, SLOTS * NC], "float32"),
+    "ps": ("psum", [128, BANKS * 512], "float32"),
+}
+for _s in range(N):
+    for _h in range(2):
+        SCRATCH["lc%d_%d" % (_h, _s)] = ("dram", [128, HW], "float8_e4m3fn_x4")
+        SCRATCH["lp%d_%d" % (_h, _s)] = ("dram", [128, HW], "uint8")
+
+SEMAPHORES = (["xl", "xr", "cpy0", "cpy1", "wl0", "wl1", "hp", "hc", "sent"]
+              + ["mm%d" % b for b in range(BANKS)]
+              + ["cp%d" % s for s in range(SLOTS)] + ["sd%d" % s for s in range(SLOTS)]
+              + ["arr%d_%d" % (h, s) for h in range(2) for s in range(N)])
+
+
+def _bits(mask):
+    return bin(mask).count("1")
+
+
+def _helper(topo, T, s, h):
+    home = T.cores[s]
+    dsts = [T.cores[(s + o) % N] for o in range(2, N)]
+    for c in range(topo.CORES_PER_CHIP * topo.CHIPS):
+        if topo.chip(c) != topo.chip(home) or c in T.cores:
+            continue
+        if (topo.die(c) == topo.die(home)) != (h == 0):
+            continue
+        if all(topo.may_write(c, d) for d in dsts):
+            return c
+    return None
+
+
+def _xfer(topo, src, dsts, cores, mask, sem):
+    ids = [DstId(rid=topo.addr(c)[0], pnc=topo.addr(c)[1]) for c in cores]
+    return RemoteDMATransfer(dst_ids=ids, dma_engine_mask=mask, remote_sem=sem, srcs=[src], dsts=dsts)
+
+
+def _codes(T, h, s):
+    return T["lc%d_%d" % (h, s)][:].bitcast(dt.uint8)
+
+
+def _plane(T, h, s):
+    return T["lp%d_%d" % (h, s)][:]
+
+
+def _helper_program(g, core, T, topo, s, h):
+    dsts = [T.cores[(s + o) % N] for o in range(2, N)]
+    mask = topo.mask(core, dsts[0])
+    for d in dsts:
+        mask &= topo.mask(core, d)
+    sem = T.sem["arr%d_%d" % (h, s)]
+    g.wait_ge(T.sem.hp, _bits(topo.mask(T.cores[s], core) & ~topo.mask(T.cores[s], T.cores[(s + 1) % N])))
+    g.remote_dma_fused([_xfer(topo, _plane(T, h, s), [_plane(T, h, s) for _ in dsts], dsts, mask, sem)],
+                       local_sem=T.sem.sent)
+    g.wait_ge(T.sem.hc, _bits(topo.mask(T.cores[s], core) & ~topo.mask(T.cores[s], T.cores[(s + 1) % N])))
+    g.remote_dma_fused([_xfer(topo, _codes(T, h, s), [_codes(T, h, s) for _ in dsts], dsts, mask, sem)],
+                       local_sem=T.sem.sent)
+    g.wait_ge(T.sem.sent, 2 * _bits(mask))
+
+
+def rank_program(g, core, T, topo):
+    rank = T.rank_of(core)
+    if rank is None:
+        for s in range(N):
+            for h in range(2):
+                if _helper(topo, T, s, h) == core:
+                    _helper_program(g, core, T, topo, s, h)
+        return
+
+    sem = T.sem
+    u8 = dt.uint8
+    for h in range(2):
+        g.sync.dma_start(_codes(T, h, rank), T.wc[:, 4 * HW * h:4 * HW * (h + 1)]).then_inc(sem["cpy%d" % h], 16)
+        g.scalar.dma_start(_plane(T, h, rank), T.ws[:, HW * h:HW * (h + 1)]).then_inc(sem["cpy%d" % h], 16)
+    g.sync.dma_start(T.xb[:], T.x[:, :]).then_inc(sem.xl, 16)
+    g.sync.dma_start(T.wq[:].bitcast(u8), T.wc[:, :]).then_inc(sem.wl0, 16)
+    g.scalar.dma_start(T.wp[:], T.ws[:, :]).then_inc(sem.wl0, 16)
+
+    succ = T.cores[(rank + 1) % N]
+    off = topo.mask(core, succ)
+    sent = 0
+    for h in range(2):
+        hel = _helper(topo, T, rank, h)
+        on = topo.mask(core, hel) & ~off
+        arr = sem["arr%d_%d" % (h, rank)]
+        g.wait_ge(sem["cpy%d" % h], 32)
+        g.remote_dma_fused([_xfer(topo, _plane(T, h, rank), [_plane(T, h, rank)], [succ], off, arr),
+                            _xfer(topo, _plane(T, h, rank), [_plane(T, h, rank)], [hel], on, sem.hp)],
+                           local_sem=sem.sent)
+        g.remote_dma_fused([_xfer(topo, _codes(T, h, rank), [_codes(T, h, rank)], [succ], off, arr),
+                            _xfer(topo, _codes(T, h, rank), [_codes(T, h, rank)], [hel], on, sem.hc)],
+                           local_sem=sem.sent)
+        sent += 2 * (_bits(off) + _bits(on))
+    g.wait_ge(sem.sent, sent)
+
+    g.vector.wait_ge(sem.xl, 16)
+    g.vector.quantize_mx(T.xq[:], T.xs[:], T.xb[:]).then_inc(sem.xr, 1)
+    g.tensor.wait_ge(sem.xr, 1)
+
+    def mm_done(q, t):
+        q.wait_ge(sem["mm%d" % (t % BANKS)], t // BANKS + 1)
+
+    for grp in range(N):
+        src = (rank - grp) % N
+        if grp:
+            for h in range(2):
+                g.sync.wait_ge(sem["arr%d_%d" % (h, src)], 2 * _bits(off))
+                mm_done(g.sync, WT * (grp - 1) + h)
+                mm_done(g.sync, WT * (grp - 1) + h + 1)
+                g.sync.dma_start(T.wq[:, HW * h:HW * (h + 1)].bitcast(u8), _codes(T, h, src)).then_inc(sem["wl%d" % h], 16)
+                g.sync.dma_start(T.wp[:, HW * h:HW * (h + 1)], _plane(T, h, src)).then_inc(sem["wl%d" % h], 16)
+        for i in range(WT):
+            t = WT * grp + i
+            b, s = t % BANKS, t % SLOTS
+            if i == 0:
+                g.tensor.wait_ge(sem.wl0, 32 * (grp + 1))
+            if i == 1 and grp:
+                g.tensor.wait_ge(sem.wl1, 32 * grp)
+            if t >= BANKS:
+                g.tensor.wait_ge(sem["cp%d" % ((t - BANKS) % SLOTS)], (t - BANKS) // SLOTS + 1)
+            g.tensor.matmul_mx(T.ps[:, 512 * b:512 * b + NC], T.wq[:, NC * i:NC * (i + 1)], T.wp[:, NC * i:NC * (i + 1)],
+                               T.xq[:], T.xs[:], True, True).then_inc(sem["mm%d" % b], 1)
+            mm_done(g.vector, t)
+            if t >= SLOTS:
+                g.vector.wait_ge(sem["sd%d" % s], 16 * (t // SLOTS))
+            g.vector.tensor_copy(T.st[:, NC * s:NC * (s + 1)], T.ps[:, 512 * b:512 * b + NC]).then_inc(sem["cp%d" % s], 1)
+            g.scalar.wait_ge(sem["cp%d" % s], t // SLOTS + 1)
+            blk = WT * src + i
+            g.scalar.dma_start(T.y[:, NC * blk:NC * (blk + 1)], T.st[:, NC * s:NC * (s + 1)]).then_inc(sem["sd%d" % s], 16)
+    total = N * WT
+    for s in range(SLOTS):
+        g.scalar.wait_ge(sem["sd%d" % s], 16 * ((total - s + SLOTS - 1) // SLOTS))

@@ -5,16 +5,17 @@ N = 7
 WT = 3
 NC = 128
 HW = WT * NC // 2
+CH = NC // 2
+WIN = NC + HW
 BANKS = 8
-SLOTS = 2
 
 SCRATCH = {
     "xb": ("sbuf", [128, 4 * NC], "bfloat16"),
     "xq": ("sbuf", [128, NC], "float8_e4m3fn_x4"),
     "xs": ("sbuf", [128, NC], "uint8"),
-    "wq": ("sbuf", [128, WT * NC], "float8_e4m3fn_x4"),
-    "wp": ("sbuf", [128, WT * NC], "uint8"),
-    "st": ("sbuf", [128, SLOTS * NC], "float32"),
+    "wq": ("sbuf", [128, WIN], "float8_e4m3fn_x4"),
+    "wp": ("sbuf", [128, WIN], "uint8"),
+    "st": ("sbuf", [128, WIN], "float32"),
     "ps": ("psum", [128, BANKS * 512], "float32"),
 }
 for _s in range(N):
@@ -22,9 +23,8 @@ for _s in range(N):
         SCRATCH["lc%d_%d" % (_h, _s)] = ("dram", [128, HW], "float8_e4m3fn_x4")
         SCRATCH["lp%d_%d" % (_h, _s)] = ("dram", [128, HW], "uint8")
 
-SEMAPHORES = (["xl", "xr", "cpy0", "cpy1", "wl0", "wl1", "hp", "hc", "sent"]
-              + ["mm%d" % b for b in range(BANKS)]
-              + ["cp%d" % s for s in range(SLOTS)] + ["sd%d" % s for s in range(SLOTS)]
+SEMAPHORES = (["xl", "xr", "cpy0", "cpy1", "wlA", "wlB", "mmA", "mmX", "mmY", "hp", "hc", "sent", "cpA", "sdA"]
+              + ["cp%d" % p for p in range(4)] + ["sd%d" % p for p in range(4)]
               + ["arr%d_%d" % (h, s) for h in range(2) for s in range(N)])
 
 
@@ -88,8 +88,8 @@ def rank_program(g, core, T, topo):
         g.sync.dma_start(_codes(T, h, rank), T.wc[:, 4 * HW * h:4 * HW * (h + 1)]).then_inc(sem["cpy%d" % h], 16)
         g.scalar.dma_start(_plane(T, h, rank), T.ws[:, HW * h:HW * (h + 1)]).then_inc(sem["cpy%d" % h], 16)
     g.sync.dma_start(T.xb[:], T.x[:, :]).then_inc(sem.xl, 16)
-    g.sync.dma_start(T.wq[:].bitcast(u8), T.wc[:, :]).then_inc(sem.wl0, 16)
-    g.scalar.dma_start(T.wp[:], T.ws[:, :]).then_inc(sem.wl0, 16)
+    g.sync.dma_start(T.wq[:, 0:NC].bitcast(u8), T.wc[:, 0:4 * NC]).then_inc(sem.wlA, 16)
+    g.scalar.dma_start(T.wp[:, 0:NC], T.ws[:, 0:NC]).then_inc(sem.wlA, 16)
 
     succ = T.cores[(rank + 1) % N]
     off = topo.mask(core, succ)
@@ -98,11 +98,13 @@ def rank_program(g, core, T, topo):
         hel = _helper(topo, T, rank, h)
         on = topo.mask(core, hel) & ~off
         arr = sem["arr%d_%d" % (h, rank)]
+        to_p = T.wp[:, NC:WIN] if h == 0 else _plane(T, h, rank)
+        to_c = T.wq[:, NC:WIN].bitcast(u8) if h == 0 else _codes(T, h, rank)
         g.wait_ge(sem["cpy%d" % h], 32)
-        g.remote_dma_fused([_xfer(topo, _plane(T, h, rank), [_plane(T, h, rank)], [succ], off, arr),
+        g.remote_dma_fused([_xfer(topo, _plane(T, h, rank), [to_p], [succ], off, arr),
                             _xfer(topo, _plane(T, h, rank), [_plane(T, h, rank)], [hel], on, sem.hp)],
                            local_sem=sem.sent)
-        g.remote_dma_fused([_xfer(topo, _codes(T, h, rank), [_codes(T, h, rank)], [succ], off, arr),
+        g.remote_dma_fused([_xfer(topo, _codes(T, h, rank), [to_c], [succ], off, arr),
                             _xfer(topo, _codes(T, h, rank), [_codes(T, h, rank)], [hel], on, sem.hc)],
                            local_sem=sem.sent)
         sent += 2 * (_bits(off) + _bits(on))
@@ -112,36 +114,91 @@ def rank_program(g, core, T, topo):
     g.vector.quantize_mx(T.xq[:], T.xs[:], T.xb[:]).then_inc(sem.xr, 1)
     g.tensor.wait_ge(sem.xr, 1)
 
-    def mm_done(q, t):
-        q.wait_ge(sem["mm%d" % (t % BANKS)], t // BANKS + 1)
+    landed = 2 * _bits(off)
+    count = {"mm": 0, "wlA": 32, "wlB": 0}
+    freed = []
 
-    for grp in range(N):
-        src = (rank - grp) % N
-        if grp:
-            for h in range(2):
-                g.sync.wait_ge(sem["arr%d_%d" % (h, src)], 2 * _bits(off))
-                mm_done(g.sync, WT * (grp - 1) + h)
-                mm_done(g.sync, WT * (grp - 1) + h + 1)
-                g.sync.dma_start(T.wq[:, HW * h:HW * (h + 1)].bitcast(u8), _codes(T, h, src)).then_inc(sem["wl%d" % h], 16)
-                g.sync.dma_start(T.wp[:, HW * h:HW * (h + 1)], _plane(T, h, src)).then_inc(sem["wl%d" % h], 16)
-        for i in range(WT):
-            t = WT * grp + i
-            b, s = t % BANKS, t % SLOTS
-            if i == 0:
-                g.tensor.wait_ge(sem.wl0, 32 * (grp + 1))
-            if i == 1 and grp:
-                g.tensor.wait_ge(sem.wl1, 32 * grp)
-            if t >= BANKS:
-                g.tensor.wait_ge(sem["cp%d" % ((t - BANKS) % SLOTS)], (t - BANKS) // SLOTS + 1)
-            g.tensor.matmul_mx(T.ps[:, 512 * b:512 * b + NC], T.wq[:, NC * i:NC * (i + 1)], T.wp[:, NC * i:NC * (i + 1)],
-                               T.xq[:], T.xs[:], True, True).then_inc(sem["mm%d" % b], 1)
-            mm_done(g.vector, t)
-            if t >= SLOTS:
-                g.vector.wait_ge(sem["sd%d" % s], 16 * (t // SLOTS))
-            g.vector.tensor_copy(T.st[:, NC * s:NC * (s + 1)], T.ps[:, 512 * b:512 * b + NC]).then_inc(sem["cp%d" % s], 1)
-            g.scalar.wait_ge(sem["cp%d" % s], t // SLOTS + 1)
-            blk = WT * src + i
-            g.scalar.dma_start(T.y[:, NC * blk:NC * (blk + 1)], T.st[:, NC * s:NC * (s + 1)]).then_inc(sem["sd%d" % s], 16)
-    total = N * WT
-    for s in range(SLOTS):
-        g.scalar.wait_ge(sem["sd%d" % s], 16 * ((total - s + SLOTS - 1) // SLOTS))
+    def back(o):
+        return (rank - o) % N
+
+    def matmul(lo, done, copies):
+        j = count["mm"]
+        count["mm"] += 1
+        if j >= BANKS:
+            for name, val in freed[j - BANKS]:
+                g.tensor.wait_ge(sem[name], val)
+        freed.append(copies)
+        c0 = 512 * (j % BANKS)
+        g.tensor.matmul_mx(T.ps[:, c0:c0 + NC], T.wq[:, lo:lo + NC], T.wp[:, lo:lo + NC],
+                           T.xq[:], T.xs[:], True, True).then_inc(sem[done], 1)
+        return c0
+
+    def piece(tag, k, p0, p1, s0, s1, ps0, rows, cols):
+        if k:
+            g.vector.wait_ge(sem["sd" + tag], 16 * k)
+        g.vector.tensor_copy(T.st[p0:p1, s0:s1], T.ps[p0:p1, ps0:ps0 + s1 - s0]).then_inc(sem["cp" + tag], 1)
+        g.scalar.wait_ge(sem["cp" + tag], k + 1)
+        g.scalar.dma_start(T.y[rows:rows + p1 - p0, cols:cols + s1 - s0], T.st[p0:p1, s0:s1]).then_inc(sem["sd" + tag], 16)
+
+    def turn_a(k, src, i):
+        if k:
+            runs = []
+            if src == rank:
+                runs.append((0, NC, T.wc[:, 4 * NC * i:4 * NC * (i + 1)], T.ws[:, NC * i:NC * (i + 1)]))
+            else:
+                a = NC * i
+                while a < NC * (i + 1):
+                    h = a // HW
+                    b = min(NC * (i + 1), HW * (h + 1))
+                    g.sync.wait_ge(sem["arr%d_%d" % (h, src)], landed)
+                    runs.append((a - NC * i, b - NC * i, T["lc%d_%d" % (h, src)][:, a - HW * h:b - HW * h].bitcast(u8),
+                                 T["lp%d_%d" % (h, src)][:, a - HW * h:b - HW * h]))
+                    a = b
+            g.sync.wait_ge(sem.mmA, k)
+            for w0, w1, cs, pl in runs:
+                g.sync.dma_start(T.wq[:, w0:w1].bitcast(u8), cs).then_inc(sem.wlA, 16)
+                g.sync.dma_start(T.wp[:, w0:w1], pl).then_inc(sem.wlA, 16)
+                count["wlA"] += 32
+        g.tensor.wait_ge(sem.wlA, count["wlA"])
+        c0 = matmul(0, "mmA", [("cpA", k + 1)])
+        g.vector.wait_ge(sem.mmA, k + 1)
+        piece("A", k, 0, 128, 0, NC, c0, 0, NC * (WT * src + i))
+
+    def turn_b(k, src, h):
+        if k:
+            g.sync.wait_ge(sem["arr%d_%d" % (h, src)], landed)
+            g.sync.wait_ge(sem.mmX, k)
+            g.sync.wait_ge(sem.mmY, k)
+            g.sync.dma_start(T.wq[:, NC:WIN].bitcast(u8), _codes(T, h, src)).then_inc(sem.wlB, 16)
+            g.sync.dma_start(T.wp[:, NC:WIN], _plane(T, h, src)).then_inc(sem.wlB, 16)
+            count["wlB"] += 32
+            g.tensor.wait_ge(sem.wlB, count["wlB"])
+        else:
+            g.tensor.wait_ge(sem["arr%d_%d" % (h, src)], landed)
+        cx = matmul(NC, "mmX", [("cp0", k + 1), ("cp3", k + 1)])
+        cy = matmul(NC + CH, "mmY", [("cp1", k + 1), ("cp2", k + 1)])
+
+        def where(j):
+            q = WT * h + j
+            return CH * (q % 2), NC * (WT * src + q // 2)
+        g.vector.wait_ge(sem.mmX, k + 1)
+        r, c = where(0)
+        piece("0", k, 0, CH, NC, 2 * NC, cx, r, c)
+        r, c = where(1)
+        piece("3", k, CH, 128, 2 * NC, WIN, cx + CH, r, c + CH)
+        g.vector.wait_ge(sem.mmY, k + 1)
+        piece("2", k, 0, CH, 2 * NC, WIN, cy, r, c)
+        r, c = where(2)
+        piece("1", k, CH, 128, NC, 2 * NC, cy, r, c)
+
+    tiles = [(back(o), i) for o in (0, 2, 5) for i in range(WT)]
+    halves = [(back(o), h) for o in (1, 3, 4, 6) for h in range(2)]
+    turn_a(0, *tiles[0])
+    turn_a(1, *tiles[1])
+    for k in range(len(halves)):
+        turn_b(k, *halves[k])
+        if k + 2 < len(tiles):
+            turn_a(k + 2, *tiles[k + 2])
+    g.scalar.wait_ge(sem.sdA, 16 * len(tiles))
+    for p in range(4):
+        g.scalar.wait_ge(sem["sd%d" % p], 16 * len(halves))

from concourse.bass import DstId, RemoteDMATransfer
from concourse.mybir import dt

N = 7
WT = 3
NC = 128
HW = WT * NC // 2
CH = NC // 2
WIN = NC + HW
BANKS = 8

SCRATCH = {
    "xb": ("sbuf", [128, 4 * NC], "bfloat16"),
    "xq": ("sbuf", [128, NC], "float8_e4m3fn_x4"),
    "xs": ("sbuf", [128, NC], "uint8"),
    "wq": ("sbuf", [128, WIN], "float8_e4m3fn_x4"),
    "wp": ("sbuf", [128, WIN], "uint8"),
    "st": ("sbuf", [128, WIN], "float32"),
    "ps": ("psum", [128, BANKS * 512], "float32"),
}
for _s in range(N):
    for _h in range(2):
        SCRATCH["lc%d_%d" % (_h, _s)] = ("dram", [128, HW], "float8_e4m3fn_x4")
        SCRATCH["lp%d_%d" % (_h, _s)] = ("dram", [128, HW], "uint8")

SEMAPHORES = (["xl", "xr", "cpy0", "cpy1", "wlA", "wlB", "mmA", "mmX", "mmY", "hp", "hc", "sent", "cpA", "sdA"]
              + ["cp%d" % p for p in range(4)] + ["sd%d" % p for p in range(4)]
              + ["arr%d_%d" % (h, s) for h in range(2) for s in range(N)])


def _bits(mask):
    return bin(mask).count("1")


def _helper(topo, T, s, h):
    home = T.cores[s]
    dsts = [T.cores[(s + o) % N] for o in range(2, N)]
    for c in range(topo.CORES_PER_CHIP * topo.CHIPS):
        if topo.chip(c) != topo.chip(home) or c in T.cores:
            continue
        if (topo.die(c) == topo.die(home)) != (h == 0):
            continue
        if all(topo.may_write(c, d) for d in dsts):
            return c
    return None


def _xfer(topo, src, dsts, cores, mask, sem):
    ids = [DstId(rid=topo.addr(c)[0], pnc=topo.addr(c)[1]) for c in cores]
    return RemoteDMATransfer(dst_ids=ids, dma_engine_mask=mask, remote_sem=sem, srcs=[src], dsts=dsts)


def _codes(T, h, s):
    return T["lc%d_%d" % (h, s)][:].bitcast(dt.uint8)


def _plane(T, h, s):
    return T["lp%d_%d" % (h, s)][:]


def _helper_program(g, core, T, topo, s, h):
    dsts = [T.cores[(s + o) % N] for o in range(2, N)]
    mask = topo.mask(core, dsts[0])
    for d in dsts:
        mask &= topo.mask(core, d)
    sem = T.sem["arr%d_%d" % (h, s)]
    g.wait_ge(T.sem.hp, _bits(topo.mask(T.cores[s], core) & ~topo.mask(T.cores[s], T.cores[(s + 1) % N])))
    g.remote_dma_fused([_xfer(topo, _plane(T, h, s), [_plane(T, h, s) for _ in dsts], dsts, mask, sem)],
                       local_sem=T.sem.sent)
    g.wait_ge(T.sem.hc, _bits(topo.mask(T.cores[s], core) & ~topo.mask(T.cores[s], T.cores[(s + 1) % N])))
    g.remote_dma_fused([_xfer(topo, _codes(T, h, s), [_codes(T, h, s) for _ in dsts], dsts, mask, sem)],
                       local_sem=T.sem.sent)
    g.wait_ge(T.sem.sent, 2 * _bits(mask))


def rank_program(g, core, T, topo):
    rank = T.rank_of(core)
    if rank is None:
        for s in range(N):
            for h in range(2):
                if _helper(topo, T, s, h) == core:
                    _helper_program(g, core, T, topo, s, h)
        return

    sem = T.sem
    u8 = dt.uint8
    for h in range(2):
        g.sync.dma_start(_codes(T, h, rank), T.wc[:, 4 * HW * h:4 * HW * (h + 1)]).then_inc(sem["cpy%d" % h], 16)
        g.scalar.dma_start(_plane(T, h, rank), T.ws[:, HW * h:HW * (h + 1)]).then_inc(sem["cpy%d" % h], 16)
    g.sync.dma_start(T.xb[:], T.x[:, :]).then_inc(sem.xl, 16)
    g.sync.dma_start(T.wq[:, 0:NC].bitcast(u8), T.wc[:, 0:4 * NC]).then_inc(sem.wlA, 16)
    g.scalar.dma_start(T.wp[:, 0:NC], T.ws[:, 0:NC]).then_inc(sem.wlA, 16)

    succ = T.cores[(rank + 1) % N]
    off = topo.mask(core, succ)
    sent = 0
    for h in range(2):
        hel = _helper(topo, T, rank, h)
        on = topo.mask(core, hel) & ~off
        arr = sem["arr%d_%d" % (h, rank)]
        to_p = T.wp[:, NC:WIN] if h == 0 else _plane(T, h, rank)
        to_c = T.wq[:, NC:WIN].bitcast(u8) if h == 0 else _codes(T, h, rank)
        g.wait_ge(sem["cpy%d" % h], 32)
        g.remote_dma_fused([_xfer(topo, _plane(T, h, rank), [to_p], [succ], off, arr),
                            _xfer(topo, _plane(T, h, rank), [_plane(T, h, rank)], [hel], on, sem.hp)],
                           local_sem=sem.sent)
        g.remote_dma_fused([_xfer(topo, _codes(T, h, rank), [to_c], [succ], off, arr),
                            _xfer(topo, _codes(T, h, rank), [_codes(T, h, rank)], [hel], on, sem.hc)],
                           local_sem=sem.sent)
        sent += 2 * (_bits(off) + _bits(on))
    g.wait_ge(sem.sent, sent)

    g.vector.wait_ge(sem.xl, 16)
    g.vector.quantize_mx(T.xq[:], T.xs[:], T.xb[:]).then_inc(sem.xr, 1)
    g.tensor.wait_ge(sem.xr, 1)

    landed = 2 * _bits(off)
    count = {"mm": 0, "wlA": 32, "wlB": 0}
    freed = []

    def back(o):
        return (rank - o) % N

    def matmul(lo, done, copies):
        j = count["mm"]
        count["mm"] += 1
        if j >= BANKS:
            for name, val in freed[j - BANKS]:
                g.tensor.wait_ge(sem[name], val)
        freed.append(copies)
        c0 = 512 * (j % BANKS)
        g.tensor.matmul_mx(T.ps[:, c0:c0 + NC], T.wq[:, lo:lo + NC], T.wp[:, lo:lo + NC],
                           T.xq[:], T.xs[:], True, True).then_inc(sem[done], 1)
        return c0

    def piece(tag, k, p0, p1, s0, s1, ps0, rows, cols):
        if k:
            g.vector.wait_ge(sem["sd" + tag], 16 * k)
        g.vector.tensor_copy(T.st[p0:p1, s0:s1], T.ps[p0:p1, ps0:ps0 + s1 - s0]).then_inc(sem["cp" + tag], 1)
        g.scalar.wait_ge(sem["cp" + tag], k + 1)
        g.scalar.dma_start(T.y[rows:rows + p1 - p0, cols:cols + s1 - s0], T.st[p0:p1, s0:s1]).then_inc(sem["sd" + tag], 16)

    def turn_a(k, src, i):
        if k:
            runs = []
            if src == rank:
                runs.append((0, NC, T.wc[:, 4 * NC * i:4 * NC * (i + 1)], T.ws[:, NC * i:NC * (i + 1)]))
            else:
                a = NC * i
                while a < NC * (i + 1):
                    h = a // HW
                    b = min(NC * (i + 1), HW * (h + 1))
                    g.sync.wait_ge(sem["arr%d_%d" % (h, src)], landed)
                    runs.append((a - NC * i, b - NC * i, T["lc%d_%d" % (h, src)][:, a - HW * h:b - HW * h].bitcast(u8),
                                 T["lp%d_%d" % (h, src)][:, a - HW * h:b - HW * h]))
                    a = b
            g.sync.wait_ge(sem.mmA, k)
            for w0, w1, cs, pl in runs:
                g.sync.dma_start(T.wq[:, w0:w1].bitcast(u8), cs).then_inc(sem.wlA, 16)
                g.sync.dma_start(T.wp[:, w0:w1], pl).then_inc(sem.wlA, 16)
                count["wlA"] += 32
        g.tensor.wait_ge(sem.wlA, count["wlA"])
        c0 = matmul(0, "mmA", [("cpA", k + 1)])
        g.vector.wait_ge(sem.mmA, k + 1)
        piece("A", k, 0, 128, 0, NC, c0, 0, NC * (WT * src + i))

    def turn_b(k, src, h):
        if k:
            g.sync.wait_ge(sem["arr%d_%d" % (h, src)], landed)
            g.sync.wait_ge(sem.mmX, k)
            g.sync.wait_ge(sem.mmY, k)
            g.sync.dma_start(T.wq[:, NC:WIN].bitcast(u8), _codes(T, h, src)).then_inc(sem.wlB, 16)
            g.sync.dma_start(T.wp[:, NC:WIN], _plane(T, h, src)).then_inc(sem.wlB, 16)
            count["wlB"] += 32
            g.tensor.wait_ge(sem.wlB, count["wlB"])
        else:
            g.tensor.wait_ge(sem["arr%d_%d" % (h, src)], landed)
        cx = matmul(NC, "mmX", [("cp0", k + 1), ("cp3", k + 1)])
        cy = matmul(NC + CH, "mmY", [("cp1", k + 1), ("cp2", k + 1)])

        def where(j):
            q = WT * h + j
            return CH * (q % 2), NC * (WT * src + q // 2)
        g.vector.wait_ge(sem.mmX, k + 1)
        r, c = where(0)
        piece("0", k, 0, CH, NC, 2 * NC, cx, r, c)
        r, c = where(1)
        piece("3", k, CH, 128, 2 * NC, WIN, cx + CH, r, c + CH)
        g.vector.wait_ge(sem.mmY, k + 1)
        piece("2", k, 0, CH, 2 * NC, WIN, cy, r, c)
        r, c = where(2)
        piece("1", k, CH, 128, NC, 2 * NC, cy, r, c)

    tiles = [(back(o), i) for o in (0, 2, 5) for i in range(WT)]
    halves = [(back(o), h) for o in (1, 3, 4, 6) for h in range(2)]
    turn_a(0, *tiles[0])
    turn_a(1, *tiles[1])
    for k in range(len(halves)):
        turn_b(k, *halves[k])
        if k + 2 < len(tiles):
            turn_a(k + 2, *tiles[k + 2])
    g.scalar.wait_ge(sem.sdA, 16 * len(tiles))
    for p in range(4):
        g.scalar.wait_ge(sem["sd%d" % p], 16 * len(halves))
